import numpy as np
import ml_dtypes


def mxq(x, axis, fmt="e4m3"):
    dtype, down = {"e4m3": (ml_dtypes.float8_e4m3fn, 7), "e5m2": (ml_dtypes.float8_e5m2, 14)}[fmt]
    v = np.moveaxis(np.asarray(x, np.float32).astype(ml_dtypes.bfloat16).astype(np.float64), axis, -1)
    blocks = v.reshape(v.shape[:-1] + (-1, 32))
    amax = np.abs(blocks).max(-1, keepdims=True)
    byte = np.maximum(np.where(amax > 0, np.frexp(amax)[1] - 1 + 127, 0) - down, 1)
    scale = np.exp2(byte - 127.0)
    codes = (blocks / scale).astype(np.float32).astype(dtype).astype(np.float64)
    return np.moveaxis((codes * scale).reshape(v.shape), -1, axis)


WIDE = False


def mx_kscale(k):
    if not WIDE:
        return np.ones(k)
    levels = np.array([10, -10, 5, -5, 0])
    if k % 512:
        return np.exp2(np.random.permutation(np.resize(levels, k // 32))).repeat(32)
    a = np.empty((k // 512, 16))
    for p in range(k // 512):
        a[p, :8] = np.random.permutation(np.resize(levels, 8))
        for g in range(8):
            far = levels[np.abs(levels - a[p, g]) >= 10]
            a[p, g + 8] = far[np.random.randint(len(far))]
    return np.exp2(a.ravel()).repeat(32)


def f64(x):
    return np.asarray(x).astype(np.float64)


def striped(idx):
    return np.tile(np.asarray(idx).reshape(-1, 16).T, (8, 1)).astype(np.uint16)


def unstriped(offs):
    return offs[:16].T.reshape(-1).astype(np.int64)


E2M1 = np.array([0.0, 0.5, 1.0, 1.5, 2.0, 3.0, 4.0, 6.0, -0.0, -0.5, -1.0, -1.5, -2.0, -3.0, -4.0, -6.0])


def pack_weight(w, fmt):
    k, n = w.shape
    w = f64(np.asarray(w, np.float32).astype(ml_dtypes.bfloat16)).reshape(k // 32, 32, n)
    amax = np.abs(w).max(1)
    if fmt == "e4m3":
        byte = np.frexp(amax)[1] - 1 + 127 - 7
    else:
        mant, ex = np.frexp(amax / 6.0)
        byte = np.where(mant > 0.5, ex, ex - 1) + 127
    byte = np.clip(np.where(amax > 0, byte, 1), 1, 254)
    scaled = (w * np.exp2(127.0 - byte)[:, None, :]).reshape(k, n).astype(np.float32)
    by_word = np.ascontiguousarray(scaled.reshape(k // 512, 128, 4, n).transpose(0, 1, 3, 2))
    if fmt == "e4m3":
        words = by_word.astype(ml_dtypes.float8_e4m3fn).view(np.uint8)
    else:
        c = by_word.astype(ml_dtypes.float4_e2m1fn).view(np.uint8) & 0xF
        words = (c[..., 0::2] | (c[..., 1::2] << 4)).reshape(k // 512, 128, 2 * n)
    return np.ascontiguousarray(words), np.ascontiguousarray(byte.astype(np.uint8).reshape(k // 512, 16, n))


def unpack_weight(words, scales, fmt):
    g, _, n = scales.shape
    words = np.ascontiguousarray(words).reshape(g, 128, n, -1)
    if fmt == "e4m3":
        vals = words.view(ml_dtypes.float8_e4m3fn).astype(np.float64)
    else:
        nib = np.empty((g, 128, n, 4), np.uint8)
        nib[..., 0::2] = words & 0xF
        nib[..., 1::2] = words >> 4
        vals = E2M1[nib]
    vals = vals * np.repeat(np.exp2(scales.astype(np.float64) - 127.0), 8, axis=1)[..., None]
    return vals.transpose(0, 1, 3, 2).reshape(g * 512, n)


def sigmoid(v):
    return 1.0 / (1.0 + np.exp(-v))


def bf(x):
    return np.asarray(x, np.float32).astype(ml_dtypes.bfloat16)


def planes(Y):
    r, m = Y.shape
    b = f64(bf(Y)).reshape(r // 32, 32, m)
    amax = np.abs(b).max(1)
    byte = np.clip(np.where(amax > 0, np.frexp(amax)[1] - 1 + 127 - 7, 1), 1, 254)
    codes = (b * np.exp2(127.0 - byte)[:, None, :]).reshape(r, m).astype(np.float32).astype(ml_dtypes.float8_e4m3fn).view(np.uint8)
    words = codes.reshape(r // 512, 128, 4, m).transpose(0, 1, 3, 2)
    return np.ascontiguousarray(words), np.ascontiguousarray(byte.astype(np.uint8).reshape(r // 512, 16, m))


K, T, J, B, N = 1024, 2048, 512, 64, 512


def setup_inputs():
    n = np.random.standard_normal
    idx = np.random.permutation(T)[:J]
    fk = mx_kscale(K)
    wvp = pack_weight(n((K, N)) * 1 / np.sqrt(K) * fk[:, None], "e2m1")
    wgp = pack_weight(n((K, N)) * 1 / np.sqrt(K) * fk[:, None], "e4m3")
    return {
        "xt": (n((K, T)) / fk[:, None]).astype(np.float32),
        "wv_words": wvp[0],
        "wv_scales": wvp[1],
        "wg_words": wgp[0],
        "wg_scales": wgp[1],
        "bw": (np.random.uniform(0.5, 2.0, (1, B))).astype(np.float32),
        "offs": striped(idx),
    }


def reference(xt, wv_words, wv_scales, wg_words, wg_scales, bw, offs):
    idx = unstriped(offs)
    wvu = unpack_weight(wv_words, wv_scales, "e2m1")
    wgu = unpack_weight(wg_words, wg_scales, "e4m3")
    xtidxq = mxq(f64(xt)[:, idx], 0, "e4m3")
    v = wvu.T @ xtidxq
    g = wgu.T @ xtidxq
    s = sigmoid(g)
    num = (s * v).reshape(N, B, J // B).sum(axis=2)
    den = s.reshape(N, B, J // B).sum(axis=2)
    y = f64(bw) * num / (den + 0.1)
    words, scales = planes(y)
    return y, words, scales

@@ -1,0 +1,225 @@
+from contextlib import ExitStack
+
+import concourse.mybir as mybir
+from concourse.masks import make_identity
+
+K, T, J, B, N = 1024, 2048, 512, 64, 512
+FLOPS = 2 * 2 * K * N * J
+
+F32 = mybir.dt.float32
+BF16 = mybir.dt.bfloat16
+I32 = mybir.dt.int32
+U32 = mybir.dt.uint32
+U16 = mybir.dt.uint16
+U8 = mybir.dt.uint8
+FP8X4 = mybir.dt.float8_e4m3fn_x4
+FP4X4 = mybir.dt.float4_e2m1fn_x4
+ACT = mybir.ActivationFunctionType
+ALU = mybir.AluOpType
+
+P = 128
+PACK = 4
+PASSES = K // (P * PACK)
+GROUP = J // B
+PAIR = P // B
+SETS = GROUP // PAIR
+QUADS = 4
+RING = 4
+WG_BYTES = N * 4
+WV_BYTES = N * 2
+
+
+def tile_list_gated_mean_of_picks_pl_kernel(
+    tc, xt, wv_words, wv_scales, wg_words, wg_scales, bw, offs, out_0, out_1, out_2
+):
+    nc = tc.nc
+    with ExitStack() as ctx:
+        keep = ctx.enter_context(tc.tile_pool(name="keep", bufs=1))
+        ring = ctx.enter_context(tc.tile_pool(name="ring", bufs=RING))
+        psum = ctx.enter_context(tc.psum_pool(name="psum", bufs=1))
+
+        x_rows = xt.rearrange("(z p t) w -> z t p w", p=P, t=PACK)
+
+        def load_rows(z, t):
+            rows = ring.tile([P, T], F32, name=f"rows{z}{t}", tag="stream", align_bytes=64)
+            nc.sync.dma_start(out=rows[:], in_=x_rows[z, t])
+            return rows
+
+        def load_weights(z):
+            words = ring.tile([P, WG_BYTES + WV_BYTES], U8, name=f"words{z}", tag="stream", align_bytes=64)
+            nc.sync.dma_start(
+                out=words[:, 0:WG_BYTES].bitcast(I32),
+                in_=wg_words[z].rearrange("p n r -> p (n r)").bitcast(I32),
+            )
+            nc.sync.dma_start(
+                out=words[:, WG_BYTES : WG_BYTES + WV_BYTES].bitcast(I32),
+                in_=wv_words[z].bitcast(I32),
+            )
+            return words
+
+        offsets = keep.tile([P, J // 16], U16, name="offsets")
+        g_scale = keep.tile([P, PASSES * N], U8, name="g_scale", align_bytes=64)
+        v_scale = keep.tile([P, PASSES * N], U8, name="v_scale", align_bytes=64)
+        bw_col = keep.tile([P, 1], F32, name="bw_col")
+        ident = keep.tile([P, P], F32, name="ident")
+
+        rows = {}
+        rows[0, 0] = load_rows(0, 0)
+        nc.sync.dma_start(offsets[:], offs)
+        for t in range(1, PACK):
+            rows[0, t] = load_rows(0, t)
+
+        for plane, src in ((g_scale, wg_scales), (v_scale, wv_scales)):
+            nc.vector.memset(plane[:].bitcast(U32), 0)
+            for q in range(QUADS):
+                nc.scalar.dma_start(
+                    out=plane[32 * q : 32 * q + 4, :].bitcast(I32).rearrange("r (z n) -> r z n", z=PASSES),
+                    in_=src[:, 4 * q : 4 * q + 4, :].bitcast(I32).rearrange("z r n -> r z n"),
+                )
+        with nc.allow_non_contiguous_dma(reason="one group weight to a partition"):
+            for h in range(PAIR):
+                nc.scalar.dma_start(out=bw_col[h:P:PAIR, :], in_=bw.rearrange("o b -> b o"))
+        make_identity(nc, ident[:])
+
+        woven = [keep.tile([P, SETS, B, PAIR, PACK], BF16, name=f"woven{z}", align_bytes=64) for z in range(PASSES)]
+        codes = {}
+        scales = {}
+
+        def gather(z, t):
+            nc.vector.tensor_copy(
+                out=woven[z][:, :, :, :, t].rearrange("p c b h -> p b c h"),
+                in_=rows[z, t][:].indirect(offsets[:]),
+            )
+
+        def quantize(z):
+            for c in range(SETS):
+                codes[z, c] = keep.tile([P, P], U32, name=f"codes{z}{c}", align_bytes=64)
+                scales[z, c] = keep.tile([P, P], U8, name=f"scales{z}{c}", align_bytes=64)
+                nc.vector.quantize_mx(
+                    out=codes[z, c][:].bitcast(FP8X4),
+                    scales=scales[z, c][:],
+                    in_=woven[z][:, c].rearrange("p b h t -> p (b h t)"),
+                )
+
+        g_bank = [psum.tile([P, N], F32, name=f"g_bank{c}", tag=f"g{c}") for c in range(SETS)]
+        v_bank = [psum.tile([P, N], F32, name=f"v_bank{c}", tag=f"v{c}") for c in range(SETS)]
+
+        def multiply(z, words):
+            for c in range(SETS):
+                for bank, w_codes, w_scale in (
+                    (g_bank[c], words[:, 0:WG_BYTES].bitcast(FP8X4), g_scale),
+                    (v_bank[c], words[:, WG_BYTES : WG_BYTES + WV_BYTES].bitcast(FP4X4), v_scale),
+                ):
+                    nc.tensor.matmul_mx(
+                        out=bank[:],
+                        lhsT=codes[z, c][:].bitcast(FP8X4),
+                        lhsT_scale=scales[z, c][:],
+                        rhs=w_codes,
+                        rhs_scale=w_scale[:, z * N : (z + 1) * N],
+                        start=(z == 0),
+                        stop=(z == PASSES - 1),
+                    )
+
+        for t in range(PACK):
+            gather(0, t)
+            if t < PACK - 1:
+                rows[1, t] = load_rows(1, t)
+        words0 = load_weights(0)
+        quantize(0)
+        multiply(0, words0)
+        gather(1, 0)
+        rows[1, PACK - 1] = load_rows(1, PACK - 1)
+        gather(1, 1)
+        words1 = load_weights(1)
+        gather(1, 2)
+        gather(1, 3)
+        quantize(1)
+        multiply(1, words1)
+
+        gate = []
+        gated = []
+        for c in range(SETS):
+            s = keep.tile([P, PACK, P], F32, name=f"gate{c}")
+            sv = keep.tile([P, PACK, P], F32, name=f"gated{c}")
+            nc.scalar.activation(out=s[:], in_=g_bank[c][:].rearrange("p (q t) -> p t q", t=PACK), func=ACT.Sigmoid)
+            nc.vector.scalar_tensor_tensor(
+                out=sv[:],
+                in0=v_bank[c][:].rearrange("p (q t) -> p t q", t=PACK),
+                scalar=bw_col[:],
+                in1=s[:],
+                op0=ALU.mult,
+                op1=ALU.mult,
+            )
+            gate.append(s)
+            gated.append(sv)
+
+        den_bank = psum.tile([P, PACK, P], F32, name="den_bank", tag="g0")
+        for c in range(SETS):
+            for t in range(PACK):
+                nc.tensor.matmul(
+                    out=den_bank[:, t, :],
+                    lhsT=gate[c][:, t, :],
+                    rhs=ident[:],
+                    is_transpose=True,
+                    start=(c == 0 and t == 0),
+                    stop=(c == SETS - 1 and t == PACK - 1),
+                )
+        den = keep.tile([P, PACK * B], F32, name="den")
+        nc.vector.tensor_reduce(
+            out=den[:],
+            in_=den_bank[:].rearrange("p t (b h) -> p (t b) h", h=PAIR),
+            axis=mybir.AxisListType.X,
+            op=ALU.add,
+        )
+        root = keep.tile([P, PACK * B], F32, name="root")
+        inv = keep.tile([P, PACK, B], F32, name="inv")
+        nc.scalar.activation(out=root[:], in_=den[:], func=ACT.Abs_reciprocal_sqrt, bias=0.1)
+        nc.scalar.activation(out=inv[:].rearrange("p t b -> p (t b)"), in_=root[:], func=ACT.Square)
+
+        num = keep.tile([P, PACK, B], F32, name="num")
+        for u in range(2):
+            num_bank = psum.tile([P, 2, P], F32, name=f"num_bank{u}", tag=f"g{1 + u}")
+            for tt in range(2):
+                for c in range(SETS):
+                    nc.tensor.matmul(
+                        out=num_bank[:, tt, :],
+                        lhsT=gated[c][:, 2 * u + tt, :],
+                        rhs=ident[:],
+                        is_transpose=True,
+                        start=(c == 0),
+                        stop=(c == SETS - 1),
+                    )
+            nc.vector.tensor_reduce(
+                out=num[:, 2 * u : 2 * u + 2, :].rearrange("p t b -> p (t b)"),
+                in_=num_bank[:].rearrange("p t (b h) -> p (t b) h", h=PAIR),
+                axis=mybir.AxisListType.X,
+                op=ALU.add,
+            )
+
+        y = keep.tile([P, PACK, B], F32, name="y")
+        y_woven = keep.tile([P, B, PACK], BF16, name="y_woven", align_bytes=64)
+        y_codes = keep.tile([P, B], U32, name="y_codes", align_bytes=64)
+        y_scales = keep.tile([P, B], U8, name="y_scales", align_bytes=64)
+        nc.vector.tensor_tensor(
+            out=y_woven[:],
+            in0=num[:].rearrange("p t b -> p b t"),
+            in1=inv[:].rearrange("p t b -> p b t"),
+            op=ALU.mult,
+        )
+        nc.vector.tensor_tensor(out=y[:], in0=num[:], in1=inv[:], op=ALU.mult)
+        nc.vector.quantize_mx(
+            out=y_codes[:].bitcast(FP8X4),
+            scales=y_scales[:],
+            in_=y_woven[:].rearrange("p b t -> p (b t)"),
+        )
+        nc.sync.dma_start(out=out_0.rearrange("(p t) b -> p t b", t=PACK), in_=y[:])
+        nc.scalar.dma_start(
+            out=out_1[0].rearrange("p b r -> p (b r)").bitcast(I32),
+            in_=y_codes[:].bitcast(I32),
+        )
+        for q in range(QUADS):
+            queue = nc.sync if q % 2 == 0 else nc.scalar
+            queue.dma_start(
+                out=out_2[0, 4 * q : 4 * q + 4, :].bitcast(I32),
+                in_=y_scales[32 * q : 32 * q + 4, :].bitcast(I32),
+            )

@@ -45,20 +45,13 @@ def tile_list_gated_mean_of_picks_pl_kernel(
             nc.sync.dma_start(out=rows[:], in_=x_rows[z, t])
             return rows
 
-        def load_weights(z):
-            words = ring.tile([P, WG_BYTES + WV_BYTES], U8, name=f"words{z}", tag="stream", align_bytes=64)
-            nc.sync.dma_start(
-                out=words[:, 0:WG_BYTES].bitcast(I32),
-                in_=wg_words[z].rearrange("p n r -> p (n r)").bitcast(I32),
-            )
-            nc.sync.dma_start(
-                out=words[:, WG_BYTES : WG_BYTES + WV_BYTES].bitcast(I32),
-                in_=wv_words[z].bitcast(I32),
-            )
-            return words
+        def load_gate_words(dst, z):
+            nc.sync.dma_start(out=dst.bitcast(I32), in_=wg_words[z].rearrange("p n r -> p (n r)").bitcast(I32))
+
+        def load_value_words(dst, z):
+            nc.sync.dma_start(out=dst.bitcast(I32), in_=wv_words[z].bitcast(I32))
 
         offsets = keep.tile([P, J // 16], U16, name="offsets")
-        g_scale = keep.tile([P, PASSES * N], U8, name="g_scale", align_bytes=64)
         v_scale = keep.tile([P, PASSES * N], U8, name="v_scale", align_bytes=64)
         bw_col = keep.tile([P, 1], F32, name="bw_col")
         ident = keep.tile([P, P], F32, name="ident")
@@ -69,16 +62,14 @@ def tile_list_gated_mean_of_picks_pl_kernel(
         for t in range(1, PACK):
             rows[0, t] = load_rows(0, t)
 
-        for plane, src in ((g_scale, wg_scales), (v_scale, wv_scales)):
-            nc.vector.memset(plane[:].bitcast(U32), 0)
+        def load_scales(plane, src):
+            nc.vector.memset(plane.bitcast(U32), 0)
             for q in range(QUADS):
                 nc.scalar.dma_start(
                     out=plane[32 * q : 32 * q + 4, :].bitcast(I32).rearrange("r (z n) -> r z n", z=PASSES),
                     in_=src[:, 4 * q : 4 * q + 4, :].bitcast(I32).rearrange("z r n -> r z n"),
                 )
-        with nc.allow_non_contiguous_dma(reason="one group weight to a partition"):
-            for h in range(PAIR):
-                nc.scalar.dma_start(out=bw_col[h:P:PAIR, :], in_=bw.rearrange("o b -> b o"))
+
         make_identity(nc, ident[:])
 
         woven = [keep.tile([P, SETS, B, PAIR, PACK], BF16, name=f"woven{z}", align_bytes=64) for z in range(PASSES)]
@@ -104,37 +95,51 @@ def tile_list_gated_mean_of_picks_pl_kernel(
         g_bank = [psum.tile([P, N], F32, name=f"g_bank{c}", tag=f"g{c}") for c in range(SETS)]
         v_bank = [psum.tile([P, N], F32, name=f"v_bank{c}", tag=f"v{c}") for c in range(SETS)]
 
-        def multiply(z, words):
-            for c in range(SETS):
-                for bank, w_codes, w_scale in (
-                    (g_bank[c], words[:, 0:WG_BYTES].bitcast(FP8X4), g_scale),
-                    (v_bank[c], words[:, WG_BYTES : WG_BYTES + WV_BYTES].bitcast(FP4X4), v_scale),
-                ):
-                    nc.tensor.matmul_mx(
-                        out=bank[:],
-                        lhsT=codes[z, c][:].bitcast(FP8X4),
-                        lhsT_scale=scales[z, c][:],
-                        rhs=w_codes,
-                        rhs_scale=w_scale[:, z * N : (z + 1) * N],
-                        start=(z == 0),
-                        stop=(z == PASSES - 1),
-                    )
+        def multiply(bank, z, c, w_codes, w_scale):
+            nc.tensor.matmul_mx(
+                out=bank[:],
+                lhsT=codes[z, c][:].bitcast(FP8X4),
+                lhsT_scale=scales[z, c][:],
+                rhs=w_codes,
+                rhs_scale=w_scale[:, z * N : (z + 1) * N],
+                start=(z == 0),
+                stop=(z == PASSES - 1),
+            )
 
         for t in range(PACK):
             gather(0, t)
             if t < PACK - 1:
                 rows[1, t] = load_rows(1, t)
-        words0 = load_weights(0)
+        early = ring.tile([P, WV_BYTES + PASSES * N], U8, name="early", tag="stream", align_bytes=64)
+        wv0 = early[:, 0:WV_BYTES]
+        g_scale = early[:, WV_BYTES : WV_BYTES + PASSES * N]
+        load_value_words(wv0, 0)
+        load_scales(v_scale[:], wv_scales)
         quantize(0)
-        multiply(0, words0)
+        for c in range(SETS):
+            multiply(v_bank[c], 0, c, wv0.bitcast(FP4X4), v_scale)
         gather(1, 0)
         rows[1, PACK - 1] = load_rows(1, PACK - 1)
         gather(1, 1)
-        words1 = load_weights(1)
+        late = ring.tile([P, 2 * WG_BYTES + WV_BYTES], U8, name="late", tag="stream", align_bytes=64)
+        wg0 = late[:, 0:WG_BYTES]
+        wg1 = late[:, WG_BYTES : 2 * WG_BYTES]
+        wv1 = late[:, 2 * WG_BYTES : 2 * WG_BYTES + WV_BYTES]
+        load_gate_words(wg0, 0)
+        load_gate_words(wg1, 1)
+        load_value_words(wv1, 1)
+        load_scales(g_scale, wg_scales)
+        with nc.allow_non_contiguous_dma(reason="one group weight to a partition"):
+            for h in range(PAIR):
+                nc.gpsimd.dma_start(out=bw_col[h:P:PAIR, :], in_=bw.rearrange("o b -> b o"))
         gather(1, 2)
         gather(1, 3)
+        for c in range(SETS):
+            multiply(g_bank[c], 0, c, wg0.bitcast(FP8X4), g_scale)
         quantize(1)
-        multiply(1, words1)
+        for c in range(SETS):
+            multiply(g_bank[c], 1, c, wg1.bitcast(FP8X4), g_scale)
+            multiply(v_bank[c], 1, c, wv1.bitcast(FP4X4), v_scale)
 
         gate = []
         gated = []
@@ -177,29 +182,35 @@ def tile_list_gated_mean_of_picks_pl_kernel(
         nc.scalar.activation(out=inv[:].rearrange("p t b -> p (t b)"), in_=root[:], func=ACT.Square)
 
         num = keep.tile([P, PACK, B], F32, name="num")
-        for u in range(2):
-            num_bank = psum.tile([P, 2, P], F32, name=f"num_bank{u}", tag=f"g{1 + u}")
-            for tt in range(2):
-                for c in range(SETS):
-                    nc.tensor.matmul(
-                        out=num_bank[:, tt, :],
-                        lhsT=gated[c][:, 2 * u + tt, :],
-                        rhs=ident[:],
-                        is_transpose=True,
-                        start=(c == 0),
-                        stop=(c == SETS - 1),
-                    )
-            nc.vector.tensor_reduce(
-                out=num[:, 2 * u : 2 * u + 2, :].rearrange("p t b -> p (t b)"),
-                in_=num_bank[:].rearrange("p t (b h) -> p (t b) h", h=PAIR),
-                axis=mybir.AxisListType.X,
-                op=ALU.add,
+        num_tags = ("g1", "g2", "g3", "v0")
+        num_bank = [psum.tile([P, P], F32, name=f"num_bank{t}", tag=num_tags[t]) for t in range(PACK)]
+
+        def add_numerator(c, t):
+            nc.tensor.matmul(
+                out=num_bank[t][:],
+                lhsT=gated[c][:, t, :],
+                rhs=ident[:],
+                is_transpose=True,
+                start=(c == 0),
+                stop=(c == SETS - 1),
             )
 
         y = keep.tile([P, PACK, B], F32, name="y")
         y_woven = keep.tile([P, B, PACK], BF16, name="y_woven", align_bytes=64)
         y_codes = keep.tile([P, B], U32, name="y_codes", align_bytes=64)
         y_scales = keep.tile([P, B], U8, name="y_scales", align_bytes=64)
+        for c in range(SETS // 2):
+            for t in range(PACK):
+                add_numerator(c, t)
+        for t in range(PACK):
+            for c in range(SETS // 2, SETS):
+                add_numerator(c, t)
+            nc.vector.tensor_reduce(
+                out=num[:, t, :],
+                in_=num_bank[t][:].rearrange("p (b h) -> p b h", h=PAIR),
+                axis=mybir.AxisListType.X,
+                op=ALU.add,
+            )
         nc.vector.tensor_tensor(
             out=y_woven[:],
             in0=num[:].rearrange("p t b -> p b t"),

@@ -24,7 +24,7 @@ GROUP = J // B
 PAIR = P // B
 SETS = GROUP // PAIR
 QUADS = 4
-RING = 4
+RING = 5
 WG_BYTES = N * 4
 WV_BYTES = N * 2
 
@@ -61,6 +61,7 @@ def tile_list_gated_mean_of_picks_pl_kernel(
         nc.sync.dma_start(offsets[:], offs)
         for t in range(1, PACK):
             rows[0, t] = load_rows(0, t)
+        rows[1, 0] = load_rows(1, 0)
 
         def load_scales(plane, src):
             nc.vector.memset(plane.bitcast(U32), 0)
@@ -71,6 +72,18 @@ def tile_list_gated_mean_of_picks_pl_kernel(
                 )
 
         make_identity(nc, ident[:])
+
+        bw_row = keep.tile([1, B], F32, name="bw_row")
+        bw_wide = keep.tile([P, P], F32, name="bw_wide")
+        bw_bank = psum.tile([P, P], F32, name="bw_bank", tag="g0")
+        nc.scalar.dma_start(out=bw_row[:], in_=bw)
+        nc.vector.memset(bw_wide[:], 0.0)
+        nc.vector.tensor_copy(
+            out=bw_wide[0:1, :].rearrange("o (b h) -> o b h", h=PAIR),
+            in_=bw_row[:].unsqueeze(2).to_broadcast([1, B, PAIR]),
+        )
+        nc.tensor.transpose(bw_bank[:], bw_wide[:], ident[:])
+        nc.vector.tensor_copy(out=bw_col[:], in_=bw_bank[:, 0:1])
 
         woven = [keep.tile([P, SETS, B, PAIR, PACK], BF16, name=f"woven{z}", align_bytes=64) for z in range(PASSES)]
         codes = {}
@@ -106,21 +119,22 @@ def tile_list_gated_mean_of_picks_pl_kernel(
                 stop=(z == PASSES - 1),
             )
 
-        for t in range(PACK):
-            gather(0, t)
-            if t < PACK - 1:
-                rows[1, t] = load_rows(1, t)
+        gather(0, 0)
+        rows[1, 1] = load_rows(1, 1)
+        gather(0, 1)
+        rows[1, 2] = load_rows(1, 2)
+        gather(0, 2)
         early = ring.tile([P, WV_BYTES + PASSES * N], U8, name="early", tag="stream", align_bytes=64)
         wv0 = early[:, 0:WV_BYTES]
         g_scale = early[:, WV_BYTES : WV_BYTES + PASSES * N]
         load_value_words(wv0, 0)
         load_scales(v_scale[:], wv_scales)
+        gather(0, 3)
+        rows[1, 3] = load_rows(1, 3)
         quantize(0)
         for c in range(SETS):
             multiply(v_bank[c], 0, c, wv0.bitcast(FP4X4), v_scale)
         gather(1, 0)
-        rows[1, PACK - 1] = load_rows(1, PACK - 1)
-        gather(1, 1)
         late = ring.tile([P, 2 * WG_BYTES + WV_BYTES], U8, name="late", tag="stream", align_bytes=64)
         wg0 = late[:, 0:WG_BYTES]
         wg1 = late[:, WG_BYTES : 2 * WG_BYTES]
@@ -129,11 +143,8 @@ def tile_list_gated_mean_of_picks_pl_kernel(
         load_gate_words(wg1, 1)
         load_value_words(wv1, 1)
         load_scales(g_scale, wg_scales)
-        with nc.allow_non_contiguous_dma(reason="one group weight to a partition"):
-            for h in range(PAIR):
-                nc.gpsimd.dma_start(out=bw_col[h:P:PAIR, :], in_=bw.rearrange("o b -> b o"))
-        gather(1, 2)
-        gather(1, 3)
+        for t in range(1, PACK):
+            gather(1, t)
         for c in range(SETS):
             multiply(g_bank[c], 0, c, wg0.bitcast(FP8X4), g_scale)
         quantize(1)
@@ -158,31 +169,36 @@ def tile_list_gated_mean_of_picks_pl_kernel(
             gate.append(s)
             gated.append(sv)
 
-        den_bank = psum.tile([P, PACK, P], F32, name="den_bank", tag="g0")
+        den_bank = [psum.tile([P, 2, P], F32, name=f"den_bank{u}", tag=f"g{u}") for u in range(2)]
         for c in range(SETS):
             for t in range(PACK):
                 nc.tensor.matmul(
-                    out=den_bank[:, t, :],
+                    out=den_bank[t // 2][:, t % 2, :],
                     lhsT=gate[c][:, t, :],
                     rhs=ident[:],
                     is_transpose=True,
-                    start=(c == 0 and t == 0),
-                    stop=(c == SETS - 1 and t == PACK - 1),
+                    start=(c == 0 and t % 2 == 0),
+                    stop=(c == SETS - 1 and t % 2 == 1),
                 )
-        den = keep.tile([P, PACK * B], F32, name="den")
-        nc.vector.tensor_reduce(
-            out=den[:],
-            in_=den_bank[:].rearrange("p t (b h) -> p (t b) h", h=PAIR),
-            axis=mybir.AxisListType.X,
-            op=ALU.add,
-        )
-        root = keep.tile([P, PACK * B], F32, name="root")
         inv = keep.tile([P, PACK, B], F32, name="inv")
-        nc.scalar.activation(out=root[:], in_=den[:], func=ACT.Abs_reciprocal_sqrt, bias=0.1)
-        nc.scalar.activation(out=inv[:].rearrange("p t b -> p (t b)"), in_=root[:], func=ACT.Square)
+        root = []
+        for u in range(2):
+            den = keep.tile([P, 2 * B], F32, name=f"den{u}")
+            root.append(keep.tile([P, 2 * B], F32, name=f"root{u}"))
+            nc.vector.tensor_reduce(
+                out=den[:],
+                in_=den_bank[u][:].rearrange("p t (b h) -> p (t b) h", h=PAIR),
+                axis=mybir.AxisListType.X,
+                op=ALU.add,
+            )
+            nc.scalar.activation(out=root[u][:], in_=den[:], func=ACT.Abs_reciprocal_sqrt, bias=0.1)
+        for u in range(2):
+            nc.scalar.activation(
+                out=inv[:, 2 * u : 2 * u + 2, :].rearrange("p t b -> p (t b)"), in_=root[u][:], func=ACT.Square
+            )
 
         num = keep.tile([P, PACK, B], F32, name="num")
-        num_tags = ("g1", "g2", "g3", "v0")
+        num_tags = ("g2", "v0", "v1", "g3")
         num_bank = [psum.tile([P, P], F32, name=f"num_bank{t}", tag=num_tags[t]) for t in range(PACK)]
 
         def add_numerator(c, t):
@@ -223,8 +239,8 @@ def tile_list_gated_mean_of_picks_pl_kernel(
             scales=y_scales[:],
             in_=y_woven[:].rearrange("p b t -> p (b t)"),
         )
-        nc.sync.dma_start(out=out_0.rearrange("(p t) b -> p t b", t=PACK), in_=y[:])
-        nc.scalar.dma_start(
+        nc.scalar.dma_start(out=out_0.rearrange("(p t) b -> p t b", t=PACK), in_=y[:])
+        nc.sync.dma_start(
             out=out_1[0].rearrange("p b r -> p (b r)").bitcast(I32),
             in_=y_codes[:].bitcast(I32),
         )

from contextlib import ExitStack

import concourse.mybir as mybir
from concourse.masks import make_identity

K, T, J, B, N = 1024, 2048, 512, 64, 512
FLOPS = 2 * 2 * K * N * J

F32 = mybir.dt.float32
BF16 = mybir.dt.bfloat16
I32 = mybir.dt.int32
U32 = mybir.dt.uint32
U16 = mybir.dt.uint16
U8 = mybir.dt.uint8
FP8X4 = mybir.dt.float8_e4m3fn_x4
FP4X4 = mybir.dt.float4_e2m1fn_x4
ACT = mybir.ActivationFunctionType
ALU = mybir.AluOpType

P = 128
PACK = 4
PASSES = K // (P * PACK)
GROUP = J // B
PAIR = P // B
SETS = GROUP // PAIR
QUADS = 4
RING = 5
WG_BYTES = N * 4
WV_BYTES = N * 2


def tile_list_gated_mean_of_picks_pl_kernel(
    tc, xt, wv_words, wv_scales, wg_words, wg_scales, bw, offs, out_0, out_1, out_2
):
    nc = tc.nc
    with ExitStack() as ctx:
        keep = ctx.enter_context(tc.tile_pool(name="keep", bufs=1))
        ring = ctx.enter_context(tc.tile_pool(name="ring", bufs=RING))
        psum = ctx.enter_context(tc.psum_pool(name="psum", bufs=1))

        x_rows = xt.rearrange("(z p t) w -> z t p w", p=P, t=PACK)

        def load_rows(z, t):
            rows = ring.tile([P, T], F32, name=f"rows{z}{t}", tag="stream", align_bytes=64)
            nc.sync.dma_start(out=rows[:], in_=x_rows[z, t])
            return rows

        def load_gate_words(dst, z):
            nc.sync.dma_start(out=dst.bitcast(I32), in_=wg_words[z].rearrange("p n r -> p (n r)").bitcast(I32))

        def load_value_words(dst, z):
            nc.sync.dma_start(out=dst.bitcast(I32), in_=wv_words[z].bitcast(I32))

        offsets = keep.tile([P, J // 16], U16, name="offsets")
        v_scale = keep.tile([P, PASSES * N], U8, name="v_scale", align_bytes=64)
        bw_col = keep.tile([P, 1], F32, name="bw_col")
        ident = keep.tile([P, P], F32, name="ident")

        rows = {}
        rows[0, 0] = load_rows(0, 0)
        nc.sync.dma_start(offsets[:], offs)
        for t in range(1, PACK):
            rows[0, t] = load_rows(0, t)
        rows[1, 0] = load_rows(1, 0)

        def load_scales(plane, src):
            nc.vector.memset(plane.bitcast(U32), 0)
            for q in range(QUADS):
                nc.scalar.dma_start(
                    out=plane[32 * q : 32 * q + 4, :].bitcast(I32).rearrange("r (z n) -> r z n", z=PASSES),
                    in_=src[:, 4 * q : 4 * q + 4, :].bitcast(I32).rearrange("z r n -> r z n"),
                )

        make_identity(nc, ident[:])

        bw_row = keep.tile([1, B], F32, name="bw_row")
        bw_wide = keep.tile([P, P], F32, name="bw_wide")
        bw_bank = psum.tile([P, P], F32, name="bw_bank", tag="g0")
        nc.scalar.dma_start(out=bw_row[:], in_=bw)
        nc.vector.memset(bw_wide[:], 0.0)
        nc.vector.tensor_copy(
            out=bw_wide[0:1, :].rearrange("o (b h) -> o b h", h=PAIR),
            in_=bw_row[:].unsqueeze(2).to_broadcast([1, B, PAIR]),
        )
        nc.tensor.transpose(bw_bank[:], bw_wide[:], ident[:])
        nc.vector.tensor_copy(out=bw_col[:], in_=bw_bank[:, 0:1])

        woven = [keep.tile([P, SETS, B, PAIR, PACK], BF16, name=f"woven{z}", align_bytes=64) for z in range(PASSES)]
        codes = {}
        scales = {}

        def gather(z, t):
            nc.vector.tensor_copy(
                out=woven[z][:, :, :, :, t].rearrange("p c b h -> p b c h"),
                in_=rows[z, t][:].indirect(offsets[:]),
            )

        def quantize(z):
            for c in range(SETS):
                codes[z, c] = keep.tile([P, P], U32, name=f"codes{z}{c}", align_bytes=64)
                scales[z, c] = keep.tile([P, P], U8, name=f"scales{z}{c}", align_bytes=64)
                nc.vector.quantize_mx(
                    out=codes[z, c][:].bitcast(FP8X4),
                    scales=scales[z, c][:],
                    in_=woven[z][:, c].rearrange("p b h t -> p (b h t)"),
                )

        g_bank = [psum.tile([P, N], F32, name=f"g_bank{c}", tag=f"g{c}") for c in range(SETS)]
        v_bank = [psum.tile([P, N], F32, name=f"v_bank{c}", tag=f"v{c}") for c in range(SETS)]

        def multiply(bank, z, c, w_codes, w_scale):
            nc.tensor.matmul_mx(
                out=bank[:],
                lhsT=codes[z, c][:].bitcast(FP8X4),
                lhsT_scale=scales[z, c][:],
                rhs=w_codes,
                rhs_scale=w_scale[:, z * N : (z + 1) * N],
                start=(z == 0),
                stop=(z == PASSES - 1),
            )

        gather(0, 0)
        rows[1, 1] = load_rows(1, 1)
        gather(0, 1)
        rows[1, 2] = load_rows(1, 2)
        gather(0, 2)
        early = ring.tile([P, WV_BYTES + PASSES * N], U8, name="early", tag="stream", align_bytes=64)
        wv0 = early[:, 0:WV_BYTES]
        g_scale = early[:, WV_BYTES : WV_BYTES + PASSES * N]
        load_value_words(wv0, 0)
        load_scales(v_scale[:], wv_scales)
        gather(0, 3)
        rows[1, 3] = load_rows(1, 3)
        quantize(0)
        for c in range(SETS):
            multiply(v_bank[c], 0, c, wv0.bitcast(FP4X4), v_scale)
        gather(1, 0)
        late = ring.tile([P, 2 * WG_BYTES + WV_BYTES], U8, name="late", tag="stream", align_bytes=64)
        wg0 = late[:, 0:WG_BYTES]
        wg1 = late[:, WG_BYTES : 2 * WG_BYTES]
        wv1 = late[:, 2 * WG_BYTES : 2 * WG_BYTES + WV_BYTES]
        load_gate_words(wg0, 0)
        load_gate_words(wg1, 1)
        load_value_words(wv1, 1)
        load_scales(g_scale, wg_scales)
        for t in range(1, PACK):
            gather(1, t)
        for c in range(SETS):
            multiply(g_bank[c], 0, c, wg0.bitcast(FP8X4), g_scale)
        quantize(1)
        for c in range(SETS):
            multiply(g_bank[c], 1, c, wg1.bitcast(FP8X4), g_scale)
            multiply(v_bank[c], 1, c, wv1.bitcast(FP4X4), v_scale)

        gate = []
        gated = []
        for c in range(SETS):
            s = keep.tile([P, PACK, P], F32, name=f"gate{c}")
            sv = keep.tile([P, PACK, P], F32, name=f"gated{c}")
            nc.scalar.activation(out=s[:], in_=g_bank[c][:].rearrange("p (q t) -> p t q", t=PACK), func=ACT.Sigmoid)
            nc.vector.scalar_tensor_tensor(
                out=sv[:],
                in0=v_bank[c][:].rearrange("p (q t) -> p t q", t=PACK),
                scalar=bw_col[:],
                in1=s[:],
                op0=ALU.mult,
                op1=ALU.mult,
            )
            gate.append(s)
            gated.append(sv)

        den_bank = [psum.tile([P, 2, P], F32, name=f"den_bank{u}", tag=f"g{u}") for u in range(2)]
        for c in range(SETS):
            for t in range(PACK):
                nc.tensor.matmul(
                    out=den_bank[t // 2][:, t % 2, :],
                    lhsT=gate[c][:, t, :],
                    rhs=ident[:],
                    is_transpose=True,
                    start=(c == 0 and t % 2 == 0),
                    stop=(c == SETS - 1 and t % 2 == 1),
                )
        inv = keep.tile([P, PACK, B], F32, name="inv")
        root = []
        for u in range(2):
            den = keep.tile([P, 2 * B], F32, name=f"den{u}")
            root.append(keep.tile([P, 2 * B], F32, name=f"root{u}"))
            nc.vector.tensor_reduce(
                out=den[:],
                in_=den_bank[u][:].rearrange("p t (b h) -> p (t b) h", h=PAIR),
                axis=mybir.AxisListType.X,
                op=ALU.add,
            )
            nc.scalar.activation(out=root[u][:], in_=den[:], func=ACT.Abs_reciprocal_sqrt, bias=0.1)
        for u in range(2):
            nc.scalar.activation(
                out=inv[:, 2 * u : 2 * u + 2, :].rearrange("p t b -> p (t b)"), in_=root[u][:], func=ACT.Square
            )

        num = keep.tile([P, PACK, B], F32, name="num")
        num_tags = ("g2", "v0", "v1", "g3")
        num_bank = [psum.tile([P, P], F32, name=f"num_bank{t}", tag=num_tags[t]) for t in range(PACK)]

        def add_numerator(c, t):
            nc.tensor.matmul(
                out=num_bank[t][:],
                lhsT=gated[c][:, t, :],
                rhs=ident[:],
                is_transpose=True,
                start=(c == 0),
                stop=(c == SETS - 1),
            )

        y = keep.tile([P, PACK, B], F32, name="y")
        y_woven = keep.tile([P, B, PACK], BF16, name="y_woven", align_bytes=64)
        y_codes = keep.tile([P, B], U32, name="y_codes", align_bytes=64)
        y_scales = keep.tile([P, B], U8, name="y_scales", align_bytes=64)
        for c in range(SETS // 2):
            for t in range(PACK):
                add_numerator(c, t)
        for t in range(PACK):
            for c in range(SETS // 2, SETS):
                add_numerator(c, t)
            nc.vector.tensor_reduce(
                out=num[:, t, :],
                in_=num_bank[t][:].rearrange("p (b h) -> p b h", h=PAIR),
                axis=mybir.AxisListType.X,
                op=ALU.add,
            )
        nc.vector.tensor_tensor(
            out=y_woven[:],
            in0=num[:].rearrange("p t b -> p b t"),
            in1=inv[:].rearrange("p t b -> p b t"),
            op=ALU.mult,
        )
        nc.vector.tensor_tensor(out=y[:], in0=num[:], in1=inv[:], op=ALU.mult)
        nc.vector.quantize_mx(
            out=y_codes[:].bitcast(FP8X4),
            scales=y_scales[:],
            in_=y_woven[:].rearrange("p b t -> p (b t)"),
        )
        nc.scalar.dma_start(out=out_0.rearrange("(p t) b -> p t b", t=PACK), in_=y[:])
        nc.sync.dma_start(
            out=out_1[0].rearrange("p b r -> p (b r)").bitcast(I32),
            in_=y_codes[:].bitcast(I32),
        )
        for q in range(QUADS):
            queue = nc.sync if q % 2 == 0 else nc.scalar
            queue.dma_start(
                out=out_2[0, 4 * q : 4 * q + 4, :].bitcast(I32),
                in_=y_scales[32 * q : 32 * q + 4, :].bitcast(I32),
            )
